import numpy as np, ml_dtypes
CORES = [2,10,50,58,66,74,122]
N = 7
import mx_ref
NC = 128
BF = ml_dtypes.bfloat16
def cut(t, i, w=512):
    return t[:, w * i:w * i + w]
def term(a, B):
    return np.stack([np.maximum(mx_ref.matmul(mx_ref.quantize(cut(a, i)), B), 0) for i in range(4)], axis=2).reshape(128, -1)
def setup_inputs(rng):
    def f(*shape):
        return mx_ref.flush((rng.standard_normal(shape, dtype=np.float32) * np.exp2(rng.integers(-2, 3, shape[:-1] + (1,)))).astype(BF))
    return {"a": f(N, 128, 4 * 512), "b": f(N, 128, 4 * NC)}
def setup_inputs_blocks(rng):
    d = setup_inputs(rng)
    for k in ("a", "b"): d[k] = mx_ref.spread(d[k], rng, 2)
    return d
def setup_inputs_wide(rng):
    d = setup_inputs(rng)
    for k in ("a", "b"): d[k] = mx_ref.flush((d[k].astype(np.float32) * np.exp2(rng.integers(-4, 5, (N, 1, 1))).astype(np.float32)).astype(BF))
    return d
def setup_inputs_lossless(rng):
    a = np.zeros((N, 128, 4 * 128, 4), np.float32)
    for r in range(N):
        k = rng.integers(0, 512, size=4 * 128)
        a[r, k // 4, np.arange(4 * 128), k % 4] = 1.0
    size = np.repeat(2.0 ** rng.integers(-4, 5, size=(1, 1, (4 * NC) // 4)), 4, axis=2)
    b = (rng.random((N, 128, 4 * NC)) < 0.8) * size
    return {"a": a.reshape(N, 128, 4 * 512).astype(BF), "b": b.astype(np.float32).astype(BF)}
def reference(a, b):
    Bq = [mx_ref.quantize(b[c]) for c in range(N)]
    y = np.zeros((N, 128, 4 * NC), np.float32)
    for c in range(N):
        y[c] = mx_ref.total([term(a[r], Bq[c]) for r in range(N)])
    return {"y": y}

@@ -1,0 +1,213 @@
+from concourse.bass import DstId, RemoteDMATransfer
+from concourse.mybir import dt, AluOpType, ActivationFunctionType
+
+W = 128
+BATCH = 2
+H_BATCHES = 2
+CODES = "float8_e4m3fn_x4"
+
+SCRATCH = {
+    "bt": ("sbuf", [128, 4 * W], "bfloat16"),
+    "at": ("sbuf", [128, 16 * W], "bfloat16"),
+    "bq": ("sbuf", [128, W], CODES),
+    "bs": ("sbuf", [128, W], "uint8"),
+    "aq": ("sbuf", [128, 4 * W], CODES),
+    "asc": ("sbuf", [128, 4 * W], "uint8"),
+    "pm": ("sbuf", [128, W], "float32"),
+    "sel": ("sbuf", [128, 16 * W], "bfloat16"),
+    "selq": ("sbuf", [128, 4 * W], CODES),
+    "sels": ("sbuf", [128, 4 * W], "uint8"),
+    "laq": ("sbuf", [128, 4 * W], CODES),
+    "las": ("sbuf", [128, 4 * W], "uint8"),
+    "lbq": ("sbuf", [128, 4 * W], CODES),
+    "lbs": ("sbuf", [128, 4 * W], "uint8"),
+    "ltq": ("sbuf", [128, 6 * W], CODES),
+    "lts": ("sbuf", [128, 6 * W], "uint8"),
+    "h": ("sbuf", [128, 16 * W], "bfloat16"),
+    "hq": ("sbuf", [128, 4 * W], CODES),
+    "hs": ("sbuf", [128, 4 * W], "uint8"),
+    "own": ("sbuf", [128, 4 * W], "float32"),
+    "yb": ("sbuf", [128, 4 * W], "float32"),
+    "ps": ("psum", [128, 8 * 512], "float32"),
+}
+SEMAPHORES = ["lb", "la0", "la1", "qb", "qa", "dif", "zs", "sl", "qs", "mo", "osc", "ove",
+              "aa", "b0", "b1", "b2", "mh0", "mh1", "hsc", "hve", "qt",
+              "t1", "t2", "t3", "t4", "t5", "t6", "sm", "vy", "st", "loc"]
+
+RELU = ActivationFunctionType.Relu
+
+
+def helper_of(rank_core, T, topo):
+    for k in range(128):
+        if topo.chip(k) == topo.chip(rank_core) and topo.die(k) != topo.die(rank_core):
+            if all(topo.may_write(k, c) for c in T.cores if c != rank_core):
+                return k
+    return None
+
+
+def dest(core, topo):
+    rid, pid, _ = topo.addr(core)
+    return DstId(rid=rid, pnc=pid)
+
+
+def engines(mask):
+    return [e for e in range(16) if mask >> e & 1]
+
+
+def bits(es):
+    return sum(1 << e for e in es)
+
+
+def cols(t, w, n=1):
+    return t[:, w * W:(w + n) * W]
+
+
+def u8(ap):
+    return ap.bitcast(dt.uint8)
+
+
+def handle(g, T, A, As, bank, b_sem, b_count, m_sem, seq, tile):
+    n = BATCH * W
+    s = BATCH * tile
+    g.tensor.wait_ge(b_sem, b_count)
+    for i in range(4):
+        o = T.ps[:, 512 * (bank + i):512 * (bank + i) + n]
+        g.tensor.matmul_mx(o, cols(A, i), cols(As, i), cols(T.lbq, s, BATCH), cols(T.lbs, s, BATCH), True, True).then_inc(m_sem, 1)
+    for i in range(4):
+        o = T.ps[:, 512 * (bank + i):512 * (bank + i) + n]
+        h = T.h[:, 4 * W * s + i:4 * W * (s + BATCH):4]
+        if i % 2 == 0:
+            g.scalar.wait_ge(m_sem, i + 1)
+            g.scalar.activation(h, o, RELU).then_inc(T.sem.hsc, 1)
+        else:
+            g.vector.wait_ge(m_sem, i + 1)
+            g.vector.tensor_scalar(h, o, 0.0, None, AluOpType.max).then_inc(T.sem.hve, 1)
+    g.vector.wait_ge(T.sem.hsc, 2 * (seq + 1))
+    g.vector.wait_ge(T.sem.hve, 2 * (seq + 1))
+    g.vector.quantize_mx(cols(T.hq, s, BATCH), cols(T.hs, s, BATCH), T.h[:, 4 * W * s:4 * W * (s + BATCH)]).then_inc(T.sem.qt, 1)
+
+
+def send_terms(g, T, topo, core, r, batch, tile, seq):
+    g.wait_ge(T.sem.qt, seq + 1)
+    N = len(T.cores)
+    es = []
+    for codes in (True, False):
+        trs = []
+        for k in range(BATCH):
+            d = BATCH * batch + k + 1
+            owner = T.cores[(r - d) % N]
+            es = engines(topo.mask(core, owner))
+            part = es[k * len(es) // BATCH:(k + 1) * len(es) // BATCH]
+            w = BATCH * tile + k
+            src, dst = (u8(cols(T.hq, w)), u8(cols(T.ltq, d - 1))) if codes else (cols(T.hs, w), cols(T.lts, d - 1))
+            trs.append(RemoteDMATransfer(dst_ids=[dest(owner, topo)], dma_engine_mask=bits(part), remote_sem=T.sem["t%d" % d], srcs=[src], dsts=[dst]))
+        g.remote_dma_fused(trs, local_sem=T.sem.loc)
+    return 2 * len(es)
+
+
+def rank_program(g, core, T, topo):
+    N = len(T.cores)
+    rank = T.rank_of(core)
+    helpers = [helper_of(c, T, topo) for c in T.cores]
+    if rank is None:
+        if core in helpers:
+            helper_program(g, core, helpers.index(core), T, topo)
+        return
+    S = T.sem
+    sent = 0
+
+    g.sync.dma_start(T.bt[:], T.b[:]).then_inc(S.lb, 16)
+    g.sync.dma_start(T.at[:, :8 * W], T.a[:, :8 * W]).then_inc(S.la0, 16)
+    g.sync.dma_start(T.at[:, 8 * W:], T.a[:, 8 * W:]).then_inc(S.la1, 16)
+
+    g.iota(T.pm[:], [[-1, W]], 0, 1, allow_small_or_imprecise_dtypes=True).then_inc(S.dif, 1)
+
+    g.vector.memset(T.sel[:], 0.0).then_inc(S.zs, 1)
+    g.vector.wait_ge(S.lb, 16)
+    g.vector.quantize_mx(T.bq[:], T.bs[:], T.bt[:]).then_inc(S.qb, 1)
+    g.vector.wait_ge(S.la0, 16)
+    g.vector.quantize_mx(cols(T.aq, 0, 2), cols(T.asc, 0, 2), T.at[:, :8 * W]).then_inc(S.qa, 1)
+    g.vector.wait_ge(S.la1, 16)
+    g.vector.quantize_mx(cols(T.aq, 2, 2), cols(T.asc, 2, 2), T.at[:, 8 * W:]).then_inc(S.qa, 1)
+    g.vector.wait_ge(S.zs, 1)
+    g.vector.wait_ge(S.dif, 1)
+    for b in range(4):
+        g.vector.tensor_scalar(T.sel[:, 4 * W * b + b:4 * W * (b + 1):4], T.pm[:], 0.0, None, AluOpType.is_equal).then_inc(S.sl, 1)
+    g.vector.wait_ge(S.sl, 4)
+    g.vector.quantize_mx(T.selq[:], T.sels[:], T.sel[:]).then_inc(S.qs, 1)
+
+    def send_b(batch):
+        ds = [BATCH * batch + k + 1 for k in range(BATCH)]
+        at_helper = batch < H_BATCHES
+        tos = [(helpers if at_helper else T.cores)[(rank + d) % N] for d in ds]
+        m = topo.mask(core, tos[0])
+        slots = [d - 1 if at_helper else d - 1 - BATCH * H_BATCHES for d in ds]
+        ids = [dest(t, topo) for t in tos]
+        sem = S["b%d" % batch]
+        g.remote_dma_fused([RemoteDMATransfer(dst_ids=ids, dma_engine_mask=m, remote_sem=sem, srcs=[u8(T.bq[:])], dsts=[u8(cols(T.lbq, s)) for s in slots])], local_sem=S.loc)
+        g.remote_dma_fused([RemoteDMATransfer(dst_ids=ids, dma_engine_mask=m, remote_sem=sem, srcs=[T.bs[:]], dsts=[cols(T.lbs, s) for s in slots])], local_sem=S.loc)
+        return 2 * len(engines(m))
+
+    away = topo.mask(core, T.cores[(rank + 1) % N])
+    mine = helpers[rank]
+    stay = topo.mask(core, mine) & ~away
+    g.wait_ge(S.qb, 1)
+    sent += send_b(0)
+    g.wait_ge(S.qa, 2)
+    rid, pid, _ = topo.addr(mine)
+    g.remote_dma(u8(T.laq[:]), u8(T.aq[:]), S.aa, S.loc, pid, rid, stay)
+    g.remote_dma(T.las[:], T.asc[:], S.aa, S.loc, pid, rid, stay)
+    sent += 2 * len(engines(stay))
+    sent += send_b(1)
+    sent += send_b(2)
+
+    g.tensor.wait_ge(S.qb, 1)
+    g.tensor.wait_ge(S.qa, 2)
+    for i in range(4):
+        g.tensor.matmul_mx(T.ps[:, 512 * (4 + i):512 * (4 + i) + W], cols(T.aq, i), cols(T.asc, i), T.bq[:], T.bs[:], True, True).then_inc(S.mo, 1)
+    for i in range(4):
+        o, t = T.ps[:, 512 * (4 + i):512 * (4 + i) + W], T.own[:, i:4 * W:4]
+        if i % 2 == 0:
+            g.scalar.wait_ge(S.mo, i + 1)
+            g.scalar.activation(t, o, RELU).then_inc(S.osc, 1)
+        else:
+            g.vector.wait_ge(S.mo, i + 1)
+            g.vector.tensor_scalar(t, o, 0.0, None, AluOpType.max).then_inc(S.ove, 1)
+
+    g.tensor.wait_ge(S.osc, 2)
+    g.tensor.wait_ge(S.ove, 2)
+    per_b = 2 * len(engines(away))
+    handle(g, T, T.aq, T.asc, 4, S["b%d" % H_BATCHES], BATCH * per_b, S.mh0, 0, 0)
+    sent += send_terms(g, T, topo, core, rank, H_BATCHES, 0, 0)
+
+    g.tensor.wait_ge(S.qs, 1)
+    per_t = per_b // BATCH
+    for d in range(1, N):
+        g.tensor.wait_ge(S["t%d" % d], per_t)
+        for b in range(4):
+            mm = g.tensor.matmul_mx(T.ps[:, 512 * b:512 * b + W], cols(T.selq, b), cols(T.sels, b), cols(T.ltq, d - 1), cols(T.lts, d - 1), d == 1, d == N - 1)
+            if d == N - 1:
+                mm.then_inc(S.sm, 1)
+    g.vector.wait_ge(S.osc, 2)
+    g.vector.wait_ge(S.ove, 2)
+    for b in range(4):
+        g.vector.wait_ge(S.sm, b + 1)
+        g.vector.tensor_tensor(T.yb[:, b:4 * W:4], T.ps[:, 512 * b:512 * b + W], T.own[:, b:4 * W:4], AluOpType.add).then_inc(S.vy, 1)
+    g.sync.wait_ge(S.vy, 4)
+    g.sync.dma_start(T.y[:], T.yb[:]).then_inc(S.st, 16)
+    g.sync.wait_ge(S.st, 16)
+    g.wait_ge(S.loc, sent)
+
+
+def helper_program(g, core, r, T, topo):
+    S = T.sem
+    N = len(T.cores)
+    owner = T.cores[r]
+    away = topo.mask(owner, T.cores[(r + 1) % N])
+    stay = topo.mask(owner, core) & ~away
+    g.tensor.wait_ge(S.aa, 2 * len(engines(stay)))
+    sent = 0
+    for batch in range(H_BATCHES):
+        handle(g, T, T.laq, T.las, 4 * batch, S["b%d" % batch], BATCH * 2 * len(engines(away)), S["mh%d" % batch], batch, batch)
+        sent += send_terms(g, T, topo, core, r, batch, batch, batch)
+    g.wait_ge(S.loc, sent)

@@ -2,9 +2,13 @@ from concourse.bass import DstId, RemoteDMATransfer
 from concourse.mybir import dt, AluOpType, ActivationFunctionType
 
 W = 128
-BATCH = 2
-H_BATCHES = 2
 CODES = "float8_e4m3fn_x4"
+
+GROUPS = [("P", [1, 2]), ("H", [3]), ("H", [4]), ("P", [5]), ("H", [6])]
+SENDS = [("codes", [[1, 2]], True), ("scales", [[1, 2]], True), ("A", [], False),
+         ("scales", [[3], [4]], False), ("codes", [[3]], False), ("codes", [[4]], False)]
+RELAYS = [("codes", [[5], [6]]), ("scales", [[5], [6]])]
+TAKE = [1, 2, 3, 4, 5, 6]
 
 SCRATCH = {
     "bt": ("sbuf", [128, 4 * W], "bfloat16"),
@@ -19,22 +23,24 @@ SCRATCH = {
     "sels": ("sbuf", [128, 4 * W], "uint8"),
     "laq": ("sbuf", [128, 4 * W], CODES),
     "las": ("sbuf", [128, 4 * W], "uint8"),
-    "lbq": ("sbuf", [128, 4 * W], CODES),
-    "lbs": ("sbuf", [128, 4 * W], "uint8"),
+    "rbq": ("sbuf", [128, W], CODES),
+    "rbs": ("sbuf", [128, W], "uint8"),
+    "lbq": ("sbuf", [128, 6 * W], CODES),
+    "lbs": ("sbuf", [128, 6 * W], "uint8"),
     "ltq": ("sbuf", [128, 6 * W], CODES),
     "lts": ("sbuf", [128, 6 * W], "uint8"),
-    "h": ("sbuf", [128, 16 * W], "bfloat16"),
-    "hq": ("sbuf", [128, 4 * W], CODES),
-    "hs": ("sbuf", [128, 4 * W], "uint8"),
-    "own": ("sbuf", [128, 4 * W], "float32"),
+    "h": ("sbuf", [128, 28 * W], "bfloat16"),
+    "hq": ("sbuf", [128, 8 * W], CODES),
+    "hs": ("sbuf", [128, 8 * W], "uint8"),
     "yb": ("sbuf", [128, 4 * W], "float32"),
     "ps": ("psum", [128, 8 * 512], "float32"),
 }
-SEMAPHORES = ["lb", "la0", "la1", "qb", "qa", "dif", "zs", "sl", "qs", "mo", "osc", "ove",
-              "aa", "b0", "b1", "b2", "mh0", "mh1", "hsc", "hve", "qt",
-              "t1", "t2", "t3", "t4", "t5", "t6", "sm", "vy", "st", "loc"]
+SEMAPHORES = ["lb", "la0", "la1", "qb", "qa", "dif", "zs", "sl", "qs",
+              "aa", "rc", "rs", "b0", "b1", "b2", "b3", "b4", "mh", "hsc", "hve", "qt",
+              "t1", "t2", "t3", "t4", "t5", "t6", "sm", "ysc", "yve", "st", "loc"]
 
 RELU = ActivationFunctionType.Relu
+COPY = ActivationFunctionType.Copy
 
 
 def helper_of(rank_core, T, topo):
@@ -66,43 +72,73 @@ def u8(ap):
     return ap.bitcast(dt.uint8)
 
 
-def handle(g, T, A, As, bank, b_sem, b_count, m_sem, seq, tile):
-    n = BATCH * W
-    s = BATCH * tile
-    g.tensor.wait_ge(b_sem, b_count)
-    for i in range(4):
-        o = T.ps[:, 512 * (bank + i):512 * (bank + i) + n]
-        g.tensor.matmul_mx(o, cols(A, i), cols(As, i), cols(T.lbq, s, BATCH), cols(T.lbs, s, BATCH), True, True).then_inc(m_sem, 1)
-    for i in range(4):
-        o = T.ps[:, 512 * (bank + i):512 * (bank + i) + n]
-        h = T.h[:, 4 * W * s + i:4 * W * (s + BATCH):4]
-        if i % 2 == 0:
-            g.scalar.wait_ge(m_sem, i + 1)
-            g.scalar.activation(h, o, RELU).then_inc(T.sem.hsc, 1)
+def group_of(d):
+    return [i for i, (_, ds) in enumerate(GROUPS) if d in ds][0]
+
+
+def share(parts, es):
+    n = len(es) // max(len(parts), 1)
+    return [(p, es[k * n:(k + 1) * n]) for k, p in enumerate(parts)]
+
+
+def arrivals(d_group, es):
+    calls = [(c[0], c[1]) for c in SENDS] + RELAYS
+    return sum(len(e) for kind, parts in calls for part, e in share(parts, es) for d in part if d in d_group)
+
+
+def b_transfers(T, topo, r, helpers, kind, parts, es, q, s):
+    trs = []
+    for part, e in share(parts, es):
+        i = group_of(part[0])
+        ids = [dest((helpers if GROUPS[i][0] == "H" else T.cores)[(r + d) % len(T.cores)], topo) for d in part]
+        src = u8(q[:]) if kind == "codes" else s[:]
+        dsts = [u8(cols(T.lbq, d - 1)) if kind == "codes" else cols(T.lbs, d - 1) for d in part]
+        trs.append(RemoteDMATransfer(dst_ids=ids, dma_engine_mask=bits(e), remote_sem=T.sem["b%d" % i], srcs=[src], dsts=dsts))
+    return trs
+
+
+def product(g, T, seq, A, As, B, Bs, s, m):
+    S = T.sem
+    if seq > 0:
+        g.tensor.wait_ge(S.hsc, 2 * seq)
+        g.tensor.wait_ge(S.hve, 2 * seq)
+    outs = [T.ps[:, 512 * (4 + k):512 * (4 + k) + m * W] for k in range(4)]
+    for k in range(4):
+        g.tensor.matmul_mx(outs[k], cols(A, k), cols(As, k), B, Bs, True, True).then_inc(S.mh, 1)
+    for k in range(4):
+        h = T.h[:, 4 * W * s + k:4 * W * (s + m):4]
+        if k % 2 == 0:
+            g.scalar.wait_ge(S.mh, 4 * seq + k + 1)
+            g.scalar.activation(h, outs[k], RELU).then_inc(S.hsc, 1)
         else:
-            g.vector.wait_ge(m_sem, i + 1)
-            g.vector.tensor_scalar(h, o, 0.0, None, AluOpType.max).then_inc(T.sem.hve, 1)
-    g.vector.wait_ge(T.sem.hsc, 2 * (seq + 1))
-    g.vector.wait_ge(T.sem.hve, 2 * (seq + 1))
-    g.vector.quantize_mx(cols(T.hq, s, BATCH), cols(T.hs, s, BATCH), T.h[:, 4 * W * s:4 * W * (s + BATCH)]).then_inc(T.sem.qt, 1)
+            g.vector.wait_ge(S.mh, 4 * seq + k + 1)
+            g.vector.tensor_scalar(h, outs[k], 0.0, None, AluOpType.max).then_inc(S.hve, 1)
+    g.vector.wait_ge(S.hsc, 2 * (seq + 1))
+    g.vector.wait_ge(S.hve, 2 * (seq + 1))
+    g.vector.quantize_mx(cols(T.hq, s, m), cols(T.hs, s, m), T.h[:, 4 * W * s:4 * W * (s + m)]).then_inc(S.qt, 1)
 
 
-def send_terms(g, T, topo, core, r, batch, tile, seq):
-    g.wait_ge(T.sem.qt, seq + 1)
+def terms(g, T, topo, core, r, who, A, As, es, seq):
+    S = T.sem
     N = len(T.cores)
-    es = []
-    for codes in (True, False):
-        trs = []
-        for k in range(BATCH):
-            d = BATCH * batch + k + 1
-            owner = T.cores[(r - d) % N]
-            es = engines(topo.mask(core, owner))
-            part = es[k * len(es) // BATCH:(k + 1) * len(es) // BATCH]
-            w = BATCH * tile + k
-            src, dst = (u8(cols(T.hq, w)), u8(cols(T.ltq, d - 1))) if codes else (cols(T.hs, w), cols(T.lts, d - 1))
-            trs.append(RemoteDMATransfer(dst_ids=[dest(owner, topo)], dma_engine_mask=bits(part), remote_sem=T.sem["t%d" % d], srcs=[src], dsts=[dst]))
-        g.remote_dma_fused(trs, local_sem=T.sem.loc)
-    return 2 * len(es)
+    sent = 0
+    for i, (w, ds) in enumerate(GROUPS):
+        if w != who:
+            continue
+        s, m = ds[0] - 1, len(ds)
+        g.tensor.wait_ge(S["b%d" % i], arrivals(ds, es))
+        product(g, T, seq, A, As, cols(T.lbq, s, m), cols(T.lbs, s, m), s, m)
+        seq += 1
+        g.wait_ge(S.qt, seq)
+        for codes in (True, False):
+            trs = []
+            for (d,), e in share([[d] for d in ds], es):
+                src, dst = (u8(cols(T.hq, d - 1)), u8(cols(T.ltq, d - 1))) if codes else (cols(T.hs, d - 1), cols(T.lts, d - 1))
+                trs.append(RemoteDMATransfer(dst_ids=[dest(T.cores[(r - d) % N], topo)], dma_engine_mask=bits(e),
+                                             remote_sem=S["t%d" % d], srcs=[src], dsts=[dst]))
+                sent += len(e)
+            g.remote_dma_fused(trs, local_sem=S.loc)
+    return sent
 
 
 def rank_program(g, core, T, topo):
@@ -111,7 +147,7 @@ def rank_program(g, core, T, topo):
     helpers = [helper_of(c, T, topo) for c in T.cores]
     if rank is None:
         if core in helpers:
-            helper_program(g, core, helpers.index(core), T, topo)
+            helper_program(g, core, helpers.index(core), helpers, T, topo)
         return
     S = T.sem
     sent = 0
@@ -136,78 +172,67 @@ def rank_program(g, core, T, topo):
     g.vector.wait_ge(S.sl, 4)
     g.vector.quantize_mx(T.selq[:], T.sels[:], T.sel[:]).then_inc(S.qs, 1)
 
-    def send_b(batch):
-        ds = [BATCH * batch + k + 1 for k in range(BATCH)]
-        at_helper = batch < H_BATCHES
-        tos = [(helpers if at_helper else T.cores)[(rank + d) % N] for d in ds]
-        m = topo.mask(core, tos[0])
-        slots = [d - 1 if at_helper else d - 1 - BATCH * H_BATCHES for d in ds]
-        ids = [dest(t, topo) for t in tos]
-        sem = S["b%d" % batch]
-        g.remote_dma_fused([RemoteDMATransfer(dst_ids=ids, dma_engine_mask=m, remote_sem=sem, srcs=[u8(T.bq[:])], dsts=[u8(cols(T.lbq, s)) for s in slots])], local_sem=S.loc)
-        g.remote_dma_fused([RemoteDMATransfer(dst_ids=ids, dma_engine_mask=m, remote_sem=sem, srcs=[T.bs[:]], dsts=[cols(T.lbs, s) for s in slots])], local_sem=S.loc)
-        return 2 * len(engines(m))
-
-    away = topo.mask(core, T.cores[(rank + 1) % N])
+    es = engines(topo.mask(core, T.cores[(rank + 1) % N]))
     mine = helpers[rank]
-    stay = topo.mask(core, mine) & ~away
+    stay = engines(topo.mask(core, mine) & ~bits(es))
     g.wait_ge(S.qb, 1)
-    sent += send_b(0)
-    g.wait_ge(S.qa, 2)
-    rid, pid, _ = topo.addr(mine)
-    g.remote_dma(u8(T.laq[:]), u8(T.aq[:]), S.aa, S.loc, pid, rid, stay)
-    g.remote_dma(T.las[:], T.asc[:], S.aa, S.loc, pid, rid, stay)
-    sent += 2 * len(engines(stay))
-    sent += send_b(1)
-    sent += send_b(2)
+    for kind, parts, to_helper in SENDS:
+        if kind == "A":
+            g.wait_ge(S.qa, 2)
+            rid, pid, _ = topo.addr(mine)
+            g.remote_dma(u8(T.laq[:]), u8(T.aq[:]), S.aa, S.loc, pid, rid, bits(stay))
+            g.remote_dma(T.las[:], T.asc[:], S.aa, S.loc, pid, rid, bits(stay))
+            sent += 2 * len(stay)
+            continue
+        trs = b_transfers(T, topo, rank, helpers, kind, parts, es, T.bq, T.bs)
+        sent += len(es)
+        if to_helper:
+            src, dst, sem = (u8(T.bq[:]), u8(T.rbq[:]), S.rc) if kind == "codes" else (T.bs[:], T.rbs[:], S.rs)
+            trs.append(RemoteDMATransfer(dst_ids=[dest(mine, topo)], dma_engine_mask=bits(stay), remote_sem=sem, srcs=[src], dsts=[dst]))
+            sent += len(stay)
+        g.remote_dma_fused(trs, local_sem=S.loc)
 
     g.tensor.wait_ge(S.qb, 1)
     g.tensor.wait_ge(S.qa, 2)
-    for i in range(4):
-        g.tensor.matmul_mx(T.ps[:, 512 * (4 + i):512 * (4 + i) + W], cols(T.aq, i), cols(T.asc, i), T.bq[:], T.bs[:], True, True).then_inc(S.mo, 1)
-    for i in range(4):
-        o, t = T.ps[:, 512 * (4 + i):512 * (4 + i) + W], T.own[:, i:4 * W:4]
-        if i % 2 == 0:
-            g.scalar.wait_ge(S.mo, i + 1)
-            g.scalar.activation(t, o, RELU).then_inc(S.osc, 1)
-        else:
-            g.vector.wait_ge(S.mo, i + 1)
-            g.vector.tensor_scalar(t, o, 0.0, None, AluOpType.max).then_inc(S.ove, 1)
-
-    g.tensor.wait_ge(S.osc, 2)
-    g.tensor.wait_ge(S.ove, 2)
-    per_b = 2 * len(engines(away))
-    handle(g, T, T.aq, T.asc, 4, S["b%d" % H_BATCHES], BATCH * per_b, S.mh0, 0, 0)
-    sent += send_terms(g, T, topo, core, rank, H_BATCHES, 0, 0)
+    product(g, T, 0, T.aq, T.asc, T.bq[:], T.bs[:], 6, 1)
+    sent += terms(g, T, topo, core, rank, "P", T.aq, T.asc, es, 1)
 
     g.tensor.wait_ge(S.qs, 1)
-    per_t = per_b // BATCH
-    for d in range(1, N):
-        g.tensor.wait_ge(S["t%d" % d], per_t)
-        for b in range(4):
-            mm = g.tensor.matmul_mx(T.ps[:, 512 * b:512 * b + W], cols(T.selq, b), cols(T.sels, b), cols(T.ltq, d - 1), cols(T.lts, d - 1), d == 1, d == N - 1)
-            if d == N - 1:
-                mm.then_inc(S.sm, 1)
-    g.vector.wait_ge(S.osc, 2)
-    g.vector.wait_ge(S.ove, 2)
+    g.tensor.wait_ge(S.qt, 1)
     for b in range(4):
-        g.vector.wait_ge(S.sm, b + 1)
-        g.vector.tensor_tensor(T.yb[:, b:4 * W:4], T.ps[:, 512 * b:512 * b + W], T.own[:, b:4 * W:4], AluOpType.add).then_inc(S.vy, 1)
-    g.sync.wait_ge(S.vy, 4)
+        g.tensor.matmul_mx(T.ps[:, 512 * b:512 * b + W], cols(T.selq, b), cols(T.sels, b), cols(T.hq, 6), cols(T.hs, 6), True, False)
+    for d in TAKE:
+        g.tensor.wait_ge(S["t%d" % d], 2 * (len(es) // len(GROUPS[group_of(d)][1])))
+        last = d == TAKE[-1]
+        for b in range(4):
+            mm = g.tensor.matmul_mx(T.ps[:, 512 * b:512 * b + W], cols(T.selq, b), cols(T.sels, b), cols(T.ltq, d - 1), cols(T.lts, d - 1), False, last)
+            if last:
+                mm.then_inc(S.sm, 1)
+    for b in range(4):
+        y, o = T.yb[:, b:4 * W:4], T.ps[:, 512 * b:512 * b + W]
+        if b % 2 == 0:
+            g.scalar.wait_ge(S.sm, b + 1)
+            g.scalar.activation(y, o, COPY).then_inc(S.ysc, 1)
+        else:
+            g.vector.wait_ge(S.sm, b + 1)
+            g.vector.tensor_copy(y, o).then_inc(S.yve, 1)
+    g.sync.wait_ge(S.ysc, 2)
+    g.sync.wait_ge(S.yve, 2)
     g.sync.dma_start(T.y[:], T.yb[:]).then_inc(S.st, 16)
     g.sync.wait_ge(S.st, 16)
     g.wait_ge(S.loc, sent)
 
 
-def helper_program(g, core, r, T, topo):
+def helper_program(g, core, r, helpers, T, topo):
     S = T.sem
-    N = len(T.cores)
     owner = T.cores[r]
-    away = topo.mask(owner, T.cores[(r + 1) % N])
-    stay = topo.mask(owner, core) & ~away
-    g.tensor.wait_ge(S.aa, 2 * len(engines(stay)))
+    es = engines(topo.mask(owner, T.cores[(r + 1) % len(T.cores)]))
+    stay = engines(topo.mask(owner, core) & ~bits(es))
     sent = 0
-    for batch in range(H_BATCHES):
-        handle(g, T, T.laq, T.las, 4 * batch, S["b%d" % batch], BATCH * 2 * len(engines(away)), S["mh%d" % batch], batch, batch)
-        sent += send_terms(g, T, topo, core, r, batch, batch, batch)
+    for kind, parts in RELAYS:
+        g.wait_ge(S.rc if kind == "codes" else S.rs, len(stay))
+        g.remote_dma_fused(b_transfers(T, topo, r, helpers, kind, parts, es, T.rbq, T.rbs), local_sem=S.loc)
+        sent += len(es)
+    g.tensor.wait_ge(S.aa, 2 * len(stay))
+    sent += terms(g, T, topo, core, r, "H", T.laq, T.las, es, 0)
     g.wait_ge(S.loc, sent)

from concourse.bass import DstId, RemoteDMATransfer
from concourse.mybir import dt, AluOpType, ActivationFunctionType

W = 128
CODES = "float8_e4m3fn_x4"

GROUPS = [("P", [1, 2]), ("H", [3]), ("H", [4]), ("P", [5]), ("H", [6])]
SENDS = [("codes", [[1, 2]], True), ("scales", [[1, 2]], True), ("A", [], False),
         ("scales", [[3], [4]], False), ("codes", [[3]], False), ("codes", [[4]], False)]
RELAYS = [("codes", [[5], [6]]), ("scales", [[5], [6]])]
TAKE = [1, 2, 3, 4, 5, 6]

SCRATCH = {
    "bt": ("sbuf", [128, 4 * W], "bfloat16"),
    "at": ("sbuf", [128, 16 * W], "bfloat16"),
    "bq": ("sbuf", [128, W], CODES),
    "bs": ("sbuf", [128, W], "uint8"),
    "aq": ("sbuf", [128, 4 * W], CODES),
    "asc": ("sbuf", [128, 4 * W], "uint8"),
    "pm": ("sbuf", [128, W], "float32"),
    "sel": ("sbuf", [128, 16 * W], "bfloat16"),
    "selq": ("sbuf", [128, 4 * W], CODES),
    "sels": ("sbuf", [128, 4 * W], "uint8"),
    "laq": ("sbuf", [128, 4 * W], CODES),
    "las": ("sbuf", [128, 4 * W], "uint8"),
    "rbq": ("sbuf", [128, W], CODES),
    "rbs": ("sbuf", [128, W], "uint8"),
    "lbq": ("sbuf", [128, 6 * W], CODES),
    "lbs": ("sbuf", [128, 6 * W], "uint8"),
    "ltq": ("sbuf", [128, 6 * W], CODES),
    "lts": ("sbuf", [128, 6 * W], "uint8"),
    "h": ("sbuf", [128, 28 * W], "bfloat16"),
    "hq": ("sbuf", [128, 8 * W], CODES),
    "hs": ("sbuf", [128, 8 * W], "uint8"),
    "yb": ("sbuf", [128, 4 * W], "float32"),
    "ps": ("psum", [128, 8 * 512], "float32"),
}
SEMAPHORES = ["lb", "la0", "la1", "qb", "qa", "dif", "zs", "sl", "qs",
              "aa", "rc", "rs", "b0", "b1", "b2", "b3", "b4", "mh", "hsc", "hve", "qt",
              "t1", "t2", "t3", "t4", "t5", "t6", "sm", "ysc", "yve", "st", "loc"]

RELU = ActivationFunctionType.Relu
COPY = ActivationFunctionType.Copy


def helper_of(rank_core, T, topo):
    for k in range(128):
        if topo.chip(k) == topo.chip(rank_core) and topo.die(k) != topo.die(rank_core):
            if all(topo.may_write(k, c) for c in T.cores if c != rank_core):
                return k
    return None


def dest(core, topo):
    rid, pid, _ = topo.addr(core)
    return DstId(rid=rid, pnc=pid)


def engines(mask):
    return [e for e in range(16) if mask >> e & 1]


def bits(es):
    return sum(1 << e for e in es)


def cols(t, w, n=1):
    return t[:, w * W:(w + n) * W]


def u8(ap):
    return ap.bitcast(dt.uint8)


def group_of(d):
    return [i for i, (_, ds) in enumerate(GROUPS) if d in ds][0]


def share(parts, es):
    n = len(es) // max(len(parts), 1)
    return [(p, es[k * n:(k + 1) * n]) for k, p in enumerate(parts)]


def arrivals(d_group, es):
    calls = [(c[0], c[1]) for c in SENDS] + RELAYS
    return sum(len(e) for kind, parts in calls for part, e in share(parts, es) for d in part if d in d_group)


def b_transfers(T, topo, r, helpers, kind, parts, es, q, s):
    trs = []
    for part, e in share(parts, es):
        i = group_of(part[0])
        ids = [dest((helpers if GROUPS[i][0] == "H" else T.cores)[(r + d) % len(T.cores)], topo) for d in part]
        src = u8(q[:]) if kind == "codes" else s[:]
        dsts = [u8(cols(T.lbq, d - 1)) if kind == "codes" else cols(T.lbs, d - 1) for d in part]
        trs.append(RemoteDMATransfer(dst_ids=ids, dma_engine_mask=bits(e), remote_sem=T.sem["b%d" % i], srcs=[src], dsts=dsts))
    return trs


def product(g, T, seq, A, As, B, Bs, s, m):
    S = T.sem
    if seq > 0:
        g.tensor.wait_ge(S.hsc, 2 * seq)
        g.tensor.wait_ge(S.hve, 2 * seq)
    outs = [T.ps[:, 512 * (4 + k):512 * (4 + k) + m * W] for k in range(4)]
    for k in range(4):
        g.tensor.matmul_mx(outs[k], cols(A, k), cols(As, k), B, Bs, True, True).then_inc(S.mh, 1)
    for k in range(4):
        h = T.h[:, 4 * W * s + k:4 * W * (s + m):4]
        if k % 2 == 0:
            g.scalar.wait_ge(S.mh, 4 * seq + k + 1)
            g.scalar.activation(h, outs[k], RELU).then_inc(S.hsc, 1)
        else:
            g.vector.wait_ge(S.mh, 4 * seq + k + 1)
            g.vector.tensor_scalar(h, outs[k], 0.0, None, AluOpType.max).then_inc(S.hve, 1)
    g.vector.wait_ge(S.hsc, 2 * (seq + 1))
    g.vector.wait_ge(S.hve, 2 * (seq + 1))
    g.vector.quantize_mx(cols(T.hq, s, m), cols(T.hs, s, m), T.h[:, 4 * W * s:4 * W * (s + m)]).then_inc(S.qt, 1)


def terms(g, T, topo, core, r, who, A, As, es, seq):
    S = T.sem
    N = len(T.cores)
    sent = 0
    for i, (w, ds) in enumerate(GROUPS):
        if w != who:
            continue
        s, m = ds[0] - 1, len(ds)
        g.tensor.wait_ge(S["b%d" % i], arrivals(ds, es))
        product(g, T, seq, A, As, cols(T.lbq, s, m), cols(T.lbs, s, m), s, m)
        seq += 1
        g.wait_ge(S.qt, seq)
        for codes in (True, False):
            trs = []
            for (d,), e in share([[d] for d in ds], es):
                src, dst = (u8(cols(T.hq, d - 1)), u8(cols(T.ltq, d - 1))) if codes else (cols(T.hs, d - 1), cols(T.lts, d - 1))
                trs.append(RemoteDMATransfer(dst_ids=[dest(T.cores[(r - d) % N], topo)], dma_engine_mask=bits(e),
                                             remote_sem=S["t%d" % d], srcs=[src], dsts=[dst]))
                sent += len(e)
            g.remote_dma_fused(trs, local_sem=S.loc)
    return sent


def rank_program(g, core, T, topo):
    N = len(T.cores)
    rank = T.rank_of(core)
    helpers = [helper_of(c, T, topo) for c in T.cores]
    if rank is None:
        if core in helpers:
            helper_program(g, core, helpers.index(core), helpers, T, topo)
        return
    S = T.sem
    sent = 0

    g.sync.dma_start(T.bt[:], T.b[:]).then_inc(S.lb, 16)
    g.sync.dma_start(T.at[:, :8 * W], T.a[:, :8 * W]).then_inc(S.la0, 16)
    g.sync.dma_start(T.at[:, 8 * W:], T.a[:, 8 * W:]).then_inc(S.la1, 16)

    g.iota(T.pm[:], [[-1, W]], 0, 1, allow_small_or_imprecise_dtypes=True).then_inc(S.dif, 1)

    g.vector.memset(T.sel[:], 0.0).then_inc(S.zs, 1)
    g.vector.wait_ge(S.lb, 16)
    g.vector.quantize_mx(T.bq[:], T.bs[:], T.bt[:]).then_inc(S.qb, 1)
    g.vector.wait_ge(S.la0, 16)
    g.vector.quantize_mx(cols(T.aq, 0, 2), cols(T.asc, 0, 2), T.at[:, :8 * W]).then_inc(S.qa, 1)
    g.vector.wait_ge(S.la1, 16)
    g.vector.quantize_mx(cols(T.aq, 2, 2), cols(T.asc, 2, 2), T.at[:, 8 * W:]).then_inc(S.qa, 1)
    g.vector.wait_ge(S.zs, 1)
    g.vector.wait_ge(S.dif, 1)
    for b in range(4):
        g.vector.tensor_scalar(T.sel[:, 4 * W * b + b:4 * W * (b + 1):4], T.pm[:], 0.0, None, AluOpType.is_equal).then_inc(S.sl, 1)
    g.vector.wait_ge(S.sl, 4)
    g.vector.quantize_mx(T.selq[:], T.sels[:], T.sel[:]).then_inc(S.qs, 1)

    es = engines(topo.mask(core, T.cores[(rank + 1) % N]))
    mine = helpers[rank]
    stay = engines(topo.mask(core, mine) & ~bits(es))
    g.wait_ge(S.qb, 1)
    for kind, parts, to_helper in SENDS:
        if kind == "A":
            g.wait_ge(S.qa, 2)
            rid, pid, _ = topo.addr(mine)
            g.remote_dma(u8(T.laq[:]), u8(T.aq[:]), S.aa, S.loc, pid, rid, bits(stay))
            g.remote_dma(T.las[:], T.asc[:], S.aa, S.loc, pid, rid, bits(stay))
            sent += 2 * len(stay)
            continue
        trs = b_transfers(T, topo, rank, helpers, kind, parts, es, T.bq, T.bs)
        sent += len(es)
        if to_helper:
            src, dst, sem = (u8(T.bq[:]), u8(T.rbq[:]), S.rc) if kind == "codes" else (T.bs[:], T.rbs[:], S.rs)
            trs.append(RemoteDMATransfer(dst_ids=[dest(mine, topo)], dma_engine_mask=bits(stay), remote_sem=sem, srcs=[src], dsts=[dst]))
            sent += len(stay)
        g.remote_dma_fused(trs, local_sem=S.loc)

    g.tensor.wait_ge(S.qb, 1)
    g.tensor.wait_ge(S.qa, 2)
    product(g, T, 0, T.aq, T.asc, T.bq[:], T.bs[:], 6, 1)
    sent += terms(g, T, topo, core, rank, "P", T.aq, T.asc, es, 1)

    g.tensor.wait_ge(S.qs, 1)
    g.tensor.wait_ge(S.qt, 1)
    for b in range(4):
        g.tensor.matmul_mx(T.ps[:, 512 * b:512 * b + W], cols(T.selq, b), cols(T.sels, b), cols(T.hq, 6), cols(T.hs, 6), True, False)
    for d in TAKE:
        g.tensor.wait_ge(S["t%d" % d], 2 * (len(es) // len(GROUPS[group_of(d)][1])))
        last = d == TAKE[-1]
        for b in range(4):
            mm = g.tensor.matmul_mx(T.ps[:, 512 * b:512 * b + W], cols(T.selq, b), cols(T.sels, b), cols(T.ltq, d - 1), cols(T.lts, d - 1), False, last)
            if last:
                mm.then_inc(S.sm, 1)
    for b in range(4):
        y, o = T.yb[:, b:4 * W:4], T.ps[:, 512 * b:512 * b + W]
        if b % 2 == 0:
            g.scalar.wait_ge(S.sm, b + 1)
            g.scalar.activation(y, o, COPY).then_inc(S.ysc, 1)
        else:
            g.vector.wait_ge(S.sm, b + 1)
            g.vector.tensor_copy(y, o).then_inc(S.yve, 1)
    g.sync.wait_ge(S.ysc, 2)
    g.sync.wait_ge(S.yve, 2)
    g.sync.dma_start(T.y[:], T.yb[:]).then_inc(S.st, 16)
    g.sync.wait_ge(S.st, 16)
    g.wait_ge(S.loc, sent)


def helper_program(g, core, r, helpers, T, topo):
    S = T.sem
    owner = T.cores[r]
    es = engines(topo.mask(owner, T.cores[(r + 1) % len(T.cores)]))
    stay = engines(topo.mask(owner, core) & ~bits(es))
    sent = 0
    for kind, parts in RELAYS:
        g.wait_ge(S.rc if kind == "codes" else S.rs, len(stay))
        g.remote_dma_fused(b_transfers(T, topo, r, helpers, kind, parts, es, T.rbq, T.rbs), local_sem=S.loc)
        sent += len(es)
    g.tensor.wait_ge(S.aa, 2 * len(stay))
    sent += terms(g, T, topo, core, r, "H", T.laq, T.las, es, 0)
    g.wait_ge(S.loc, sent)
